import numpy as np
import ml_dtypes


def mxq(x, axis, fmt="e4m3"):
    dtype, down = {"e4m3": (ml_dtypes.float8_e4m3fn, 7), "e5m2": (ml_dtypes.float8_e5m2, 14)}[fmt]
    v = np.moveaxis(np.asarray(x, np.float32).astype(ml_dtypes.bfloat16).astype(np.float64), axis, -1)
    blocks = v.reshape(v.shape[:-1] + (-1, 32))
    amax = np.abs(blocks).max(-1, keepdims=True)
    byte = np.maximum(np.where(amax > 0, np.frexp(amax)[1] - 1 + 127, 0) - down, 1)
    scale = np.exp2(byte - 127.0)
    codes = (blocks / scale).astype(np.float32).astype(dtype).astype(np.float64)
    return np.moveaxis((codes * scale).reshape(v.shape), -1, axis)


WIDE = False


def mx_kscale(k):
    if not WIDE:
        return np.ones(k)
    levels = np.array([10, -10, 5, -5, 0])
    if k % 512:
        return np.exp2(np.random.permutation(np.resize(levels, k // 32))).repeat(32)
    a = np.empty((k // 512, 16))
    for p in range(k // 512):
        a[p, :8] = np.random.permutation(np.resize(levels, 8))
        for g in range(8):
            far = levels[np.abs(levels - a[p, g]) >= 10]
            a[p, g + 8] = far[np.random.randint(len(far))]
    return np.exp2(a.ravel()).repeat(32)


def f64(x):
    return np.asarray(x).astype(np.float64)


def striped(idx):
    return np.tile(idx.reshape(-1, 16).T, (8, 1)).astype(np.uint16)


def unstriped(offs):
    return offs[:16].T.reshape(-1).astype(np.int64)


def striped8(idx):
    return np.concatenate([x.reshape(-1, 16).T for x in idx]).astype(np.uint16)


def runs(offs, k):
    lists = np.stack([offs[16 * r : 16 * r + 16].T.reshape(-1) for r in range(8)]).astype(np.int64)
    return lists[np.arange(k) % 512 // 64]


def pack_weight(w):
    k, n = w.shape
    w = f64(np.asarray(w, np.float32).astype(ml_dtypes.bfloat16)).reshape(k // 32, 32, n)
    amax = np.abs(w).max(1)
    byte = np.clip(np.where(amax > 0, np.frexp(amax)[1] - 1 + 127 - 7, 1), 1, 254)
    scaled = (w * np.exp2(127.0 - byte)[:, None, :]).reshape(k, n).astype(np.float32)
    words = np.ascontiguousarray(scaled.reshape(k // 512, 128, 4, n).transpose(0, 1, 3, 2)).astype(ml_dtypes.float8_e4m3fn).view(np.uint8)
    return words, np.ascontiguousarray(byte.astype(np.uint8).reshape(k // 512, 16, n))


def unpack_weight(words, scales):
    g, p, n, _ = words.shape
    vals = np.ascontiguousarray(words).view(ml_dtypes.float8_e4m3fn).astype(np.float64) * np.repeat(np.exp2(scales.astype(np.float64) - 127.0), 8, axis=1)[..., None]
    return vals.transpose(0, 1, 3, 2).reshape(g * 512, n)

def planes(y):
    n, m = y.shape
    v = y.astype(np.float32).astype(ml_dtypes.bfloat16).astype(np.float64).reshape(n // 32, 32, m)
    top = np.abs(v).max(1)
    byte = np.clip(np.where(top > 0, np.frexp(top)[1] - 1 + 127 - 7, 1), 1, 254)
    codes = (v * np.exp2(127.0 - byte)[:, None, :]).reshape(n, m).astype(np.float32).astype(ml_dtypes.float8_e4m3fn).view(np.uint8)
    words = codes.reshape(n // 512, 128, 4, m).transpose(0, 1, 3, 2)
    return np.ascontiguousarray(words), np.ascontiguousarray(byte.astype(np.uint8).reshape(n // 512, 16, m))


K, T, S, G, H, C, U = 512, 1024, 256, 2048, 512, 512, 512


def setup_inputs():
    n = np.random.standard_normal
    s = mx_kscale(K)[:, None]
    packed_xT = pack_weight(n((K, T)) * s)
    packed_dT = pack_weight(n((K, G)) / s)
    perm = np.random.permutation(U)
    return {
        "x_words": packed_xT[0],
        "x_scales": packed_xT[1],
        "d_words": packed_dT[0],
        "d_scales": packed_dT[1],
        "gs": (np.random.uniform(0.5, 1.5, (K, 1)) / s).astype(np.float32),
        "offs": striped(np.random.permutation(T)[:S]),
        "k1": striped8(np.random.randint(0, G, (8, H))),
        "n1": striped(np.random.permutation(S)),
        "n2": striped(np.random.permutation(S)),
        "cand": striped8(np.random.randint(0, T, (8, C))),
        "n3": striped(perm[:S]),
        "n4": striped(perm[S:]),
        "n5": striped(np.random.permutation(S)),
    }


def reference(x_words, x_scales, d_words, d_scales, gs, offs, k1, n1, n2, cand, n3, n4, n5):
    x_cand = unpack_weight(x_words, x_scales)[np.arange(K)[:, None], runs(cand, K)]
    d_k1 = unpack_weight(d_words, d_scales)[np.arange(K)[:, None], runs(k1, K)]
    xq = unpack_weight(x_words, x_scales)[:, unstriped(offs)]
    h = 0.0625 * (d_k1.T @ xq)
    ds = np.zeros((H, S))
    ds[:, unstriped(n1)] = h
    z = f64(gs) * (np.maximum(h, ds[:, unstriped(n2)]))
    s = 0.0625 * ((x_cand.T @ mxq(z, 0, "e4m3")))
    nw = s - s[:, unstriped(n5)]
    ph = np.zeros((C, U))
    ph[:, unstriped(n3)] = s
    out = ph.copy()
    out[:, unstriped(n4)] = nw
    return (out,) + planes(out)

@@ -1,0 +1,191 @@
+from contextlib import ExitStack
+
+import concourse.mybir as mybir
+
+F32 = mybir.dt.float32
+BF16 = mybir.dt.bfloat16
+I32 = mybir.dt.int32
+U32 = mybir.dt.uint32
+U16 = mybir.dt.uint16
+U8 = mybir.dt.uint8
+FP8X4 = mybir.dt.float8_e4m3fn_x4
+ALU = mybir.AluOpType
+COPY = mybir.ActivationFunctionType.Copy
+
+P = 128
+PACK = 4
+K, T, S, G, H, C, U = 512, 1024, 256, 2048, 512, 512, 512
+FLOPS = 2 * K * H * S + 2 * K * C * S
+LANES = 16
+HALVES = ((0, 128), (128, 256))
+Z_CHUNKS = ((0, 64), (64, 128), (128, 256))
+PAGE_SPLIT = 256
+FINISH_ORDER = (2, 0, 1, 3)
+
+
+def entries(lst, a, b):
+    return lst[:, a // LANES : b // LANES]
+
+
+def tile_picked_pqhcrelaypagq_none_po_kernel(
+    tc, x_words, x_scales, d_words, d_scales, gs, offs, k1, n1, n2, cand, n3, n4, n5, out_0, out_1, out_2
+):
+    nc = tc.nc
+    with ExitStack() as ctx:
+        keep = ctx.enter_context(tc.tile_pool(name="keep", bufs=1))
+        psum = ctx.enter_context(tc.psum_pool(name="psum", bufs=8))
+
+        def load_list(src, name):
+            lst = keep.tile(list(src.shape), U16, name=name)
+            nc.sync.dma_start(lst[:], src)
+            return lst
+
+        def load_words(src, width, name):
+            words = keep.tile([P, width], U32, name=name, align_bytes=64)
+            nc.sync.dma_start(words[:].bitcast(I32), src[0].rearrange("p n t -> p (n t)").bitcast(I32))
+            return words
+
+        def zeroed_bytes(engine, width, name):
+            tile = keep.tile([P, width], U8, name=name, align_bytes=64)
+            engine.memset(tile[:].bitcast(I32), 0)
+            return tile
+
+        d_scale_table = keep.tile([P, G], U8, name="d_scale_table", align_bytes=64)
+        x_scale_table = keep.tile([P, T], U8, name="x_scale_table", align_bytes=64)
+        d_plane = zeroed_bytes(nc.gpsimd, H, "d_plane")
+        c_plane = zeroed_bytes(nc.gpsimd, C, "c_plane")
+
+        k1_l = load_list(k1, "k1_l")
+        nc.sync.dma_start(
+            d_scale_table[:].bitcast(I32), d_scales[0].bitcast(I32).unsqueeze(1).to_broadcast([16, 8, G // 4])
+        )
+        offs_l = load_list(offs, "offs_l")
+        n1_l = load_list(n1, "n1_l")
+        d_table = load_words(d_words, G, "d_table")
+        x_rows = x_scales[0].bitcast(I32)
+        for q in range(4):
+            nc.sync.dma_start(
+                x_scale_table[32 * q : 32 * q + 32, :].bitcast(I32),
+                x_rows[4 * q : 4 * q + 4, :].unsqueeze(0).to_broadcast([8, 4, T // 4]),
+            )
+        cand_l = load_list(cand, "cand_l")
+        n2_l = load_list(n2, "n2_l")
+        x_table = load_words(x_words, T, "x_table")
+        n3_l = load_list(n3, "n3_l")
+        n5_l = load_list(n5, "n5_l")
+        n4_l = load_list(n4, "n4_l")
+        gain = keep.tile([P, PACK], F32, name="gain")
+        nc.gpsimd.dma_start(gain[:], gs.rearrange("(p t) o -> p (t o)", t=PACK))
+        sixteenth = keep.tile([P, 1], F32, name="sixteenth", tag="larger2")
+        nc.vector.memset(sixteenth[:], 0.0625)
+
+        def picked_scales(table, lst, rows, plane, name, tag):
+            picked = keep.tile([P, H], U8, name=name + "_picked", tag=tag, align_bytes=64)
+            nc.vector.tensor_copy(picked[:], table[:].indirect(lst[:]))
+            for i in range(4):
+                nc.sync.dma_start(plane[i:P:32, :].bitcast(I32), picked[rows[i] : P : 32, :].bitcast(I32))
+
+        def picked_words(table, lst, name, tag):
+            picked = keep.tile([P, H], U32, name=name + "_picked", tag=tag, align_bytes=64)
+            nc.vector.tensor_copy(picked[:], table[:].indirect(lst[:]))
+            return picked
+
+        def deal(picked, plane, t, name):
+            words = keep.tile([P, P], U32, name=name + "_words%d" % t, align_bytes=64)
+            nc.vector.tensor_copy(words[:], picked[:, t : H : PACK])
+            scales = keep.tile([P, P], U8, name=name + "_scales%d" % t, align_bytes=64)
+            nc.vector.tensor_copy(scales[:], plane[:, t : H : PACK])
+            return words, scales
+
+        def product(dest, stationary, rhs_words, rhs_plane, factor=0.0625):
+            acc = psum.tile([P, dest.shape[1]], F32, name="acc")
+            nc.tensor.matmul_mx(
+                acc[:], lhsT=stationary[0][:].bitcast(FP8X4), lhsT_scale=stationary[1][:],
+                rhs=rhs_words.bitcast(FP8X4), rhs_scale=rhs_plane, start=True, stop=True,
+            )
+            nc.vector.tensor_scalar(dest, acc[:], factor, None, ALU.mult)
+
+        xq_words = keep.tile([P, S], U32, name="xq_words", tag="x_picked_words", align_bytes=64)
+        xq_plane = keep.tile([P, S], U8, name="xq_plane", tag="x_picked_scales", align_bytes=64)
+        h = keep.tile([P, PACK, S], F32, name="h")
+        ds = [keep.tile([P, S], F32, name="ds%d" % t) for t in range(PACK)]
+
+        picked_scales(d_scale_table, k1_l, (0, 8, 16, 24), d_plane, "d_scales", "d_picked_scales")
+        d_dealt = []
+        for a, b in HALVES:
+            nc.vector.tensor_copy(xq_plane[:, a:b], x_scale_table[:].indirect(entries(offs_l, a, b)))
+            if a == 0:
+                d_picked = picked_words(d_table, k1_l, "d_words", "d_picked_words")
+            nc.vector.tensor_copy(xq_words[:, a:b], x_table[:].indirect(entries(offs_l, a, b)))
+            for t in range(PACK):
+                if a == 0:
+                    d_dealt.append(deal(d_picked, d_plane, t, "d_dealt"))
+                product(h[:, t, a:b], d_dealt[t], xq_words[:, a:b], xq_plane[:, a:b])
+                nc.scalar.activation(ds[t][:].indirect(entries(n1_l, a, b)), h[:, t, a:b], COPY)
+
+        picked_scales(x_scale_table, cand_l, (0, 1, 18, 19), c_plane, "c_scales", "x_picked_scales")
+        c_picked = picked_words(x_table, cand_l, "c_words", "x_picked_words")
+        c_dealt = [deal(c_picked, c_plane, t, "c_dealt") for t in range(PACK)]
+
+        fetched = keep.tile([P, PACK, S], F32, name="fetched")
+        z = keep.tile([P, S, PACK], BF16, name="z", align_bytes=64)
+        z_words = keep.tile([P, S], U32, name="z_words", align_bytes=64)
+        z_plane = keep.tile([P, S], U8, name="z_plane", align_bytes=64)
+        s = [keep.tile([P, S], F32, name="s%d" % t) for t in range(PACK)]
+        page = [keep.tile([P, U], F32, name="page%d" % t) for t in range(PACK)]
+        for j, (a, b) in enumerate(Z_CHUNKS):
+            larger = keep.tile([P, PACK, b - a], F32, name="larger%d" % j)
+            for t in range(PACK):
+                nc.scalar.activation(fetched[:, t, a:b], ds[t][:].indirect(entries(n2_l, a, b)), COPY)
+            nc.vector.tensor_tensor(larger[:], h[:, :, a:b], fetched[:, :, a:b], ALU.max)
+            nc.vector.tensor_tensor(
+                z[:, a:b, :].rearrange("p (c i) t -> p c t i", i=4),
+                larger[:].rearrange("p t (c i) -> p c t i", i=4),
+                gain[:].unsqueeze(1).unsqueeze(3).to_broadcast([P, (b - a) // 4, PACK, 4]),
+                ALU.mult,
+            )
+            nc.vector.quantize_mx(
+                z_words[:, a:b].bitcast(FP8X4), z_plane[:, a:b], z[:, a:b, :].rearrange("p c t -> p (c t)")
+            )
+            for t in FINISH_ORDER:
+                product(s[t][:, a:b], c_dealt[t], z_words[:, a:b], z_plane[:, a:b], sixteenth[:] if j == 0 else 0.0625)
+
+        for a, b in Z_CHUNKS[:-1]:
+            for t in range(PACK):
+                nc.scalar.activation(page[t][:].indirect(entries(n3_l, a, b)), s[t][:, a:b], COPY)
+
+        partner = [keep.tile([P, S], F32, name="partner%d" % t) for t in range(PACK)]
+        nw = [keep.tile([P, S], F32, name="nw%d" % t) for t in range(PACK)]
+        left = keep.tile([P, PAGE_SPLIT, PACK], BF16, name="left", align_bytes=64)
+        right = keep.tile([P, U - PAGE_SPLIT, PACK], BF16, name="right", align_bytes=64)
+        out_rows = out_0.rearrange("(p t) c -> p t c", t=PACK)
+
+        def finish(t):
+            nc.scalar.activation(page[t][:].indirect(n4_l[:]), nw[t][:], COPY)
+            nc.sync.dma_start(out_rows[:, t, :], page[t][:])
+            if t == PACK - 1:
+                nc.scalar.copy(right[:, :, t], page[t][:, PAGE_SPLIT:U])
+            else:
+                nc.vector.tensor_copy(right[:, :, t], page[t][:, PAGE_SPLIT:U])
+            nc.vector.tensor_copy(left[:, :, t], page[t][:, 0:PAGE_SPLIT])
+
+        a, b = Z_CHUNKS[-1]
+        for n, t in enumerate(FINISH_ORDER):
+            nc.scalar.activation(page[t][:].indirect(entries(n3_l, a, b)), s[t][:, a:b], COPY)
+            for c, d in HALVES:
+                nc.scalar.activation(partner[t][:, c:d], s[t][:].indirect(entries(n5_l, c, d)), COPY)
+            nc.vector.tensor_tensor(nw[t][:], s[t][:], partner[t][:], ALU.subtract)
+            if n > 0:
+                finish(FINISH_ORDER[n - 1])
+        finish(PACK - 1)
+
+        o_words = keep.tile([P, U], U32, name="o_words", align_bytes=64)
+        o_plane = keep.tile([P, U], U8, name="o_plane", align_bytes=64)
+        word_rows = out_1[0].rearrange("p n t -> p (n t)").bitcast(I32)
+        for part, a, b in ((left, 0, PAGE_SPLIT), (right, PAGE_SPLIT, U)):
+            nc.vector.quantize_mx(o_words[:, a:b].bitcast(FP8X4), o_plane[:, a:b], part[:].rearrange("p c t -> p (c t)"))
+            nc.sync.dma_start(word_rows[:, a:b], o_words[:, a:b].bitcast(I32))
+        scale_rows = out_2[0].bitcast(I32)
+        for q in range(4):
+            queue = nc.scalar if q % 2 == 0 else nc.sync
+            queue.dma_start(scale_rows[4 * q : 4 * q + 4, :], o_plane[32 * q : 32 * q + 4, :].bitcast(I32))

@@ -42,65 +42,68 @@ def tile_picked_pqhcrelaypagq_none_po_kernel(
 
         def load_words(src, width, name):
             words = keep.tile([P, width], U32, name=name, align_bytes=64)
-            nc.sync.dma_start(words[:].bitcast(I32), src[0].rearrange("p n t -> p (n t)").bitcast(I32))
+            nc.scalar.dma_start(words[:].bitcast(I32), src[0].rearrange("p n t -> p (n t)").bitcast(I32))
             return words
+
+        def load_scales(queue, src, width, name, tag):
+            table = keep.tile([P, width], U8, name=name, tag=tag, align_bytes=64)
+            rows = src[0].bitcast(I32).unsqueeze(1).to_broadcast([16, 8, width // 4])
+            queue.dma_start(table[:].bitcast(I32), rows)
+            return table
 
         def zeroed_bytes(engine, width, name):
             tile = keep.tile([P, width], U8, name=name, align_bytes=64)
             engine.memset(tile[:].bitcast(I32), 0)
             return tile
 
-        d_scale_table = keep.tile([P, G], U8, name="d_scale_table", align_bytes=64)
-        x_scale_table = keep.tile([P, T], U8, name="x_scale_table", align_bytes=64)
-        d_plane = zeroed_bytes(nc.gpsimd, H, "d_plane")
-        c_plane = zeroed_bytes(nc.gpsimd, C, "c_plane")
+        d_plane = zeroed_bytes(nc.vector, H, "d_plane")
+        c_plane = zeroed_bytes(nc.vector, C, "c_plane")
 
+        xq_scale_table = zeroed_bytes(nc.vector, T, "xq_scale_table")
+        x_rows = keep.tile([4, 4, T // 4], I32, name="x_rows")
+        gain = keep.tile([P, PACK], F32, name="gain")
+        nc.gpsimd.dma_start(gain[:], gs.rearrange("(p t) o -> p (t o)", t=PACK))
         k1_l = load_list(k1, "k1_l")
-        nc.sync.dma_start(
-            d_scale_table[:].bitcast(I32), d_scales[0].bitcast(I32).unsqueeze(1).to_broadcast([16, 8, G // 4])
-        )
+        nc.scalar.dma_start(x_rows[:], x_scales[0].bitcast(I32).rearrange("(q i) c -> i q c", i=4))
+        d_scale_table = load_scales(nc.scalar, d_scales, G, "d_scale_table", "d_scale_table")
         offs_l = load_list(offs, "offs_l")
-        n1_l = load_list(n1, "n1_l")
         d_table = load_words(d_words, G, "d_table")
-        x_rows = x_scales[0].bitcast(I32)
-        for q in range(4):
-            nc.sync.dma_start(
-                x_scale_table[32 * q : 32 * q + 32, :].bitcast(I32),
-                x_rows[4 * q : 4 * q + 4, :].unsqueeze(0).to_broadcast([8, 4, T // 4]),
-            )
+        n1_l = load_list(n1, "n1_l")
         cand_l = load_list(cand, "cand_l")
         n2_l = load_list(n2, "n2_l")
         x_table = load_words(x_words, T, "x_table")
         n3_l = load_list(n3, "n3_l")
         n5_l = load_list(n5, "n5_l")
         n4_l = load_list(n4, "n4_l")
-        gain = keep.tile([P, PACK], F32, name="gain")
-        nc.gpsimd.dma_start(gain[:], gs.rearrange("(p t) o -> p (t o)", t=PACK))
         sixteenth = keep.tile([P, 1], F32, name="sixteenth", tag="larger2")
         nc.vector.memset(sixteenth[:], 0.0625)
+        first_sixteenth = keep.tile([P, 1], F32, name="first_sixteenth", tag="d_dealt_late", align_bytes=64)
+        nc.vector.memset(first_sixteenth[:], 0.0625)
 
-        def picked_scales(table, lst, rows, plane, name, tag):
+        def picked_scales(table, lst, plane, queue, name, tag):
             picked = keep.tile([P, H], U8, name=name + "_picked", tag=tag, align_bytes=64)
             nc.vector.tensor_copy(picked[:], table[:].indirect(lst[:]))
+            dealt = keep.tile([P, H], U8, name=name + "_dealt", align_bytes=64)
+            nc.vector.tensor_copy(
+                dealt[:].rearrange("p (t m) -> p t m", t=PACK), picked[:].rearrange("p (m t) -> p t m", t=PACK)
+            )
             for i in range(4):
-                nc.sync.dma_start(plane[i:P:32, :].bitcast(I32), picked[rows[i] : P : 32, :].bitcast(I32))
+                queue.dma_start(plane[i:P:32, :].bitcast(I32), dealt[8 * i : P : 32, :].bitcast(I32))
 
         def picked_words(table, lst, name, tag):
             picked = keep.tile([P, H], U32, name=name + "_picked", tag=tag, align_bytes=64)
             nc.vector.tensor_copy(picked[:], table[:].indirect(lst[:]))
             return picked
 
-        def deal(picked, plane, t, name):
-            words = keep.tile([P, P], U32, name=name + "_words%d" % t, align_bytes=64)
-            nc.vector.tensor_copy(words[:], picked[:, t : H : PACK])
-            scales = keep.tile([P, P], U8, name=name + "_scales%d" % t, align_bytes=64)
-            nc.vector.tensor_copy(scales[:], plane[:, t : H : PACK])
-            return words, scales
+        def deal(picked, plane, t0, t1, name):
+            words = keep.tile([P, t1 - t0, P], U32, name=name, align_bytes=64)
+            nc.vector.tensor_copy(words[:], picked[:].rearrange("p (m t) -> p t m", t=PACK)[:, t0:t1, :])
+            return [(words[:, t - t0, :], plane[:, P * t : P * (t + 1)]) for t in range(t0, t1)]
 
         def product(dest, stationary, rhs_words, rhs_plane, factor=0.0625):
             acc = psum.tile([P, dest.shape[1]], F32, name="acc")
             nc.tensor.matmul_mx(
-                acc[:], lhsT=stationary[0][:].bitcast(FP8X4), lhsT_scale=stationary[1][:],
+                acc[:], lhsT=stationary[0].bitcast(FP8X4), lhsT_scale=stationary[1],
                 rhs=rhs_words.bitcast(FP8X4), rhs_scale=rhs_plane, start=True, stop=True,
             )
             nc.vector.tensor_scalar(dest, acc[:], factor, None, ALU.mult)
@@ -110,22 +113,28 @@ def tile_picked_pqhcrelaypagq_none_po_kernel(
         h = keep.tile([P, PACK, S], F32, name="h")
         ds = [keep.tile([P, S], F32, name="ds%d" % t) for t in range(PACK)]
 
-        picked_scales(d_scale_table, k1_l, (0, 8, 16, 24), d_plane, "d_scales", "d_picked_scales")
+        picked_scales(d_scale_table, k1_l, d_plane, nc.sync, "d_scales", "d_picked_scales")
+        for q in range(4):
+            nc.vector.tensor_copy(xq_scale_table[32 * q : 32 * q + 4, :].bitcast(I32), x_rows[:, q, :])
         d_dealt = []
         for a, b in HALVES:
-            nc.vector.tensor_copy(xq_plane[:, a:b], x_scale_table[:].indirect(entries(offs_l, a, b)))
+            nc.vector.tensor_copy(xq_plane[:, a:b], xq_scale_table[:].indirect(entries(offs_l, a, b)))
             if a == 0:
                 d_picked = picked_words(d_table, k1_l, "d_words", "d_picked_words")
             nc.vector.tensor_copy(xq_words[:, a:b], x_table[:].indirect(entries(offs_l, a, b)))
             for t in range(PACK):
-                if a == 0:
-                    d_dealt.append(deal(d_picked, d_plane, t, "d_dealt"))
-                product(h[:, t, a:b], d_dealt[t], xq_words[:, a:b], xq_plane[:, a:b])
+                if a == 0 and t < 2:
+                    d_dealt.extend(deal(d_picked, d_plane, t, t + 1, "d_dealt%d" % t))
+                if a == 0 and t == 2:
+                    d_dealt.extend(deal(d_picked, d_plane, 2, PACK, "d_dealt_late"))
+                factor = first_sixteenth[:] if (a, t) == (0, 0) else 0.0625
+                product(h[:, t, a:b], d_dealt[t], xq_words[:, a:b], xq_plane[:, a:b], factor)
                 nc.scalar.activation(ds[t][:].indirect(entries(n1_l, a, b)), h[:, t, a:b], COPY)
 
-        picked_scales(x_scale_table, cand_l, (0, 1, 18, 19), c_plane, "c_scales", "x_picked_scales")
+        x_scale_table = load_scales(nc.sync, x_scales, T, "x_scale_table", "d_table")
+        picked_scales(x_scale_table, cand_l, c_plane, nc.sync, "c_scales", "x_picked_scales")
         c_picked = picked_words(x_table, cand_l, "c_words", "x_picked_words")
-        c_dealt = [deal(c_picked, c_plane, t, "c_dealt") for t in range(PACK)]
+        c_dealt = deal(c_picked, c_plane, 0, PACK, "c_dealt")
 
         fetched = keep.tile([P, PACK, S], F32, name="fetched")
         z = keep.tile([P, S, PACK], BF16, name="z", align_bytes=64)

@@ -77,15 +77,13 @@ def tile_picked_pqhcrelaypagq_none_po_kernel(
         n4_l = load_list(n4, "n4_l")
         sixteenth = keep.tile([P, 1], F32, name="sixteenth", tag="larger2")
         nc.vector.memset(sixteenth[:], 0.0625)
-        first_sixteenth = keep.tile([P, 1], F32, name="first_sixteenth", tag="d_dealt_late", align_bytes=64)
-        nc.vector.memset(first_sixteenth[:], 0.0625)
 
         def picked_scales(table, lst, plane, queue, name, tag):
             picked = keep.tile([P, H], U8, name=name + "_picked", tag=tag, align_bytes=64)
             nc.vector.tensor_copy(picked[:], table[:].indirect(lst[:]))
             dealt = keep.tile([P, H], U8, name=name + "_dealt", align_bytes=64)
             nc.vector.tensor_copy(
-                dealt[:].rearrange("p (t m) -> p t m", t=PACK), picked[:].rearrange("p (m t) -> p t m", t=PACK)
+                dealt[:].rearrange("p (t m) -> p m t", t=PACK), picked[:].rearrange("p (m t) -> p m t", t=PACK)
             )
             for i in range(4):
                 queue.dma_start(plane[i:P:32, :].bitcast(I32), dealt[8 * i : P : 32, :].bitcast(I32))
@@ -95,10 +93,10 @@ def tile_picked_pqhcrelaypagq_none_po_kernel(
             nc.vector.tensor_copy(picked[:], table[:].indirect(lst[:]))
             return picked
 
-        def deal(picked, plane, t0, t1, name):
-            words = keep.tile([P, t1 - t0, P], U32, name=name, align_bytes=64)
-            nc.vector.tensor_copy(words[:], picked[:].rearrange("p (m t) -> p t m", t=PACK)[:, t0:t1, :])
-            return [(words[:, t - t0, :], plane[:, P * t : P * (t + 1)]) for t in range(t0, t1)]
+        def deal(picked, plane, name):
+            words = keep.tile([P, PACK, P], U32, name=name, align_bytes=64)
+            nc.vector.tensor_copy(words[:].rearrange("p t m -> p m t"), picked[:].rearrange("p (m t) -> p m t", t=PACK))
+            return [(words[:, t, :], plane[:, P * t : P * (t + 1)]) for t in range(PACK)]
 
         def product(dest, stationary, rhs_words, rhs_plane, factor=0.0625):
             acc = psum.tile([P, dest.shape[1]], F32, name="acc")
@@ -116,25 +114,20 @@ def tile_picked_pqhcrelaypagq_none_po_kernel(
         picked_scales(d_scale_table, k1_l, d_plane, nc.sync, "d_scales", "d_picked_scales")
         for q in range(4):
             nc.vector.tensor_copy(xq_scale_table[32 * q : 32 * q + 4, :].bitcast(I32), x_rows[:, q, :])
-        d_dealt = []
         for a, b in HALVES:
             nc.vector.tensor_copy(xq_plane[:, a:b], xq_scale_table[:].indirect(entries(offs_l, a, b)))
             if a == 0:
                 d_picked = picked_words(d_table, k1_l, "d_words", "d_picked_words")
+                d_dealt = deal(d_picked, d_plane, "d_dealt")
             nc.vector.tensor_copy(xq_words[:, a:b], x_table[:].indirect(entries(offs_l, a, b)))
             for t in range(PACK):
-                if a == 0 and t < 2:
-                    d_dealt.extend(deal(d_picked, d_plane, t, t + 1, "d_dealt%d" % t))
-                if a == 0 and t == 2:
-                    d_dealt.extend(deal(d_picked, d_plane, 2, PACK, "d_dealt_late"))
-                factor = first_sixteenth[:] if (a, t) == (0, 0) else 0.0625
-                product(h[:, t, a:b], d_dealt[t], xq_words[:, a:b], xq_plane[:, a:b], factor)
+                product(h[:, t, a:b], d_dealt[t], xq_words[:, a:b], xq_plane[:, a:b])
                 nc.scalar.activation(ds[t][:].indirect(entries(n1_l, a, b)), h[:, t, a:b], COPY)
 
         x_scale_table = load_scales(nc.sync, x_scales, T, "x_scale_table", "d_table")
         picked_scales(x_scale_table, cand_l, c_plane, nc.sync, "c_scales", "x_picked_scales")
         c_picked = picked_words(x_table, cand_l, "c_words", "x_picked_words")
-        c_dealt = deal(c_picked, c_plane, 0, PACK, "c_dealt")
+        c_dealt = deal(c_picked, c_plane, "c_dealt")
 
         fetched = keep.tile([P, PACK, S], F32, name="fetched")
         z = keep.tile([P, S, PACK], BF16, name="z", align_bytes=64)
@@ -146,7 +139,7 @@ def tile_picked_pqhcrelaypagq_none_po_kernel(
             larger = keep.tile([P, PACK, b - a], F32, name="larger%d" % j)
             for t in range(PACK):
                 nc.scalar.activation(fetched[:, t, a:b], ds[t][:].indirect(entries(n2_l, a, b)), COPY)
-            nc.vector.tensor_tensor(larger[:], h[:, :, a:b], fetched[:, :, a:b], ALU.max)
+                nc.vector.tensor_tensor(larger[:, t, :], h[:, t, a:b], fetched[:, t, a:b], ALU.max)
             nc.vector.tensor_tensor(
                 z[:, a:b, :].rearrange("p (c i) t -> p c t i", i=4),
                 larger[:].rearrange("p t (c i) -> p c t i", i=4),

@@ -139,7 +139,7 @@ def tile_picked_pqhcrelaypagq_none_po_kernel(
             larger = keep.tile([P, PACK, b - a], F32, name="larger%d" % j)
             for t in range(PACK):
                 nc.scalar.activation(fetched[:, t, a:b], ds[t][:].indirect(entries(n2_l, a, b)), COPY)
-                nc.vector.tensor_tensor(larger[:, t, :], h[:, t, a:b], fetched[:, t, a:b], ALU.max)
+            nc.vector.tensor_tensor(larger[:], h[:, :, a:b], fetched[:, :, a:b], ALU.max)
             nc.vector.tensor_tensor(
                 z[:, a:b, :].rearrange("p (c i) t -> p c t i", i=4),
                 larger[:].rearrange("p t (c i) -> p c t i", i=4),

from contextlib import ExitStack

import concourse.mybir as mybir

F32 = mybir.dt.float32
BF16 = mybir.dt.bfloat16
I32 = mybir.dt.int32
U32 = mybir.dt.uint32
U16 = mybir.dt.uint16
U8 = mybir.dt.uint8
FP8X4 = mybir.dt.float8_e4m3fn_x4
ALU = mybir.AluOpType
COPY = mybir.ActivationFunctionType.Copy

P = 128
PACK = 4
K, T, S, G, H, C, U = 512, 1024, 256, 2048, 512, 512, 512
FLOPS = 2 * K * H * S + 2 * K * C * S
LANES = 16
HALVES = ((0, 128), (128, 256))
Z_CHUNKS = ((0, 64), (64, 128), (128, 256))
PAGE_SPLIT = 256
FINISH_ORDER = (2, 0, 1, 3)


def entries(lst, a, b):
    return lst[:, a // LANES : b // LANES]


def tile_picked_pqhcrelaypagq_none_po_kernel(
    tc, x_words, x_scales, d_words, d_scales, gs, offs, k1, n1, n2, cand, n3, n4, n5, out_0, out_1, out_2
):
    nc = tc.nc
    with ExitStack() as ctx:
        keep = ctx.enter_context(tc.tile_pool(name="keep", bufs=1))
        psum = ctx.enter_context(tc.psum_pool(name="psum", bufs=8))

        def load_list(src, name):
            lst = keep.tile(list(src.shape), U16, name=name)
            nc.sync.dma_start(lst[:], src)
            return lst

        def load_words(src, width, name):
            words = keep.tile([P, width], U32, name=name, align_bytes=64)
            nc.scalar.dma_start(words[:].bitcast(I32), src[0].rearrange("p n t -> p (n t)").bitcast(I32))
            return words

        def load_scales(queue, src, width, name, tag):
            table = keep.tile([P, width], U8, name=name, tag=tag, align_bytes=64)
            rows = src[0].bitcast(I32).unsqueeze(1).to_broadcast([16, 8, width // 4])
            queue.dma_start(table[:].bitcast(I32), rows)
            return table

        def zeroed_bytes(engine, width, name):
            tile = keep.tile([P, width], U8, name=name, align_bytes=64)
            engine.memset(tile[:].bitcast(I32), 0)
            return tile

        d_plane = zeroed_bytes(nc.vector, H, "d_plane")
        c_plane = zeroed_bytes(nc.vector, C, "c_plane")

        xq_scale_table = zeroed_bytes(nc.vector, T, "xq_scale_table")
        x_rows = keep.tile([4, 4, T // 4], I32, name="x_rows")
        gain = keep.tile([P, PACK], F32, name="gain")
        nc.gpsimd.dma_start(gain[:], gs.rearrange("(p t) o -> p (t o)", t=PACK))
        k1_l = load_list(k1, "k1_l")
        nc.scalar.dma_start(x_rows[:], x_scales[0].bitcast(I32).rearrange("(q i) c -> i q c", i=4))
        d_scale_table = load_scales(nc.scalar, d_scales, G, "d_scale_table", "d_scale_table")
        offs_l = load_list(offs, "offs_l")
        d_table = load_words(d_words, G, "d_table")
        n1_l = load_list(n1, "n1_l")
        cand_l = load_list(cand, "cand_l")
        n2_l = load_list(n2, "n2_l")
        x_table = load_words(x_words, T, "x_table")
        n3_l = load_list(n3, "n3_l")
        n5_l = load_list(n5, "n5_l")
        n4_l = load_list(n4, "n4_l")
        sixteenth = keep.tile([P, 1], F32, name="sixteenth", tag="larger2")
        nc.vector.memset(sixteenth[:], 0.0625)

        def picked_scales(table, lst, plane, queue, name, tag):
            picked = keep.tile([P, H], U8, name=name + "_picked", tag=tag, align_bytes=64)
            nc.vector.tensor_copy(picked[:], table[:].indirect(lst[:]))
            dealt = keep.tile([P, H], U8, name=name + "_dealt", align_bytes=64)
            nc.vector.tensor_copy(
                dealt[:].rearrange("p (t m) -> p m t", t=PACK), picked[:].rearrange("p (m t) -> p m t", t=PACK)
            )
            for i in range(4):
                queue.dma_start(plane[i:P:32, :].bitcast(I32), dealt[8 * i : P : 32, :].bitcast(I32))

        def picked_words(table, lst, name, tag):
            picked = keep.tile([P, H], U32, name=name + "_picked", tag=tag, align_bytes=64)
            nc.vector.tensor_copy(picked[:], table[:].indirect(lst[:]))
            return picked

        def deal(picked, plane, name):
            words = keep.tile([P, PACK, P], U32, name=name, align_bytes=64)
            nc.vector.tensor_copy(words[:].rearrange("p t m -> p m t"), picked[:].rearrange("p (m t) -> p m t", t=PACK))
            return [(words[:, t, :], plane[:, P * t : P * (t + 1)]) for t in range(PACK)]

        def product(dest, stationary, rhs_words, rhs_plane, factor=0.0625):
            acc = psum.tile([P, dest.shape[1]], F32, name="acc")
            nc.tensor.matmul_mx(
                acc[:], lhsT=stationary[0].bitcast(FP8X4), lhsT_scale=stationary[1],
                rhs=rhs_words.bitcast(FP8X4), rhs_scale=rhs_plane, start=True, stop=True,
            )
            nc.vector.tensor_scalar(dest, acc[:], factor, None, ALU.mult)

        xq_words = keep.tile([P, S], U32, name="xq_words", tag="x_picked_words", align_bytes=64)
        xq_plane = keep.tile([P, S], U8, name="xq_plane", tag="x_picked_scales", align_bytes=64)
        h = keep.tile([P, PACK, S], F32, name="h")
        ds = [keep.tile([P, S], F32, name="ds%d" % t) for t in range(PACK)]

        picked_scales(d_scale_table, k1_l, d_plane, nc.sync, "d_scales", "d_picked_scales")
        for q in range(4):
            nc.vector.tensor_copy(xq_scale_table[32 * q : 32 * q + 4, :].bitcast(I32), x_rows[:, q, :])
        for a, b in HALVES:
            nc.vector.tensor_copy(xq_plane[:, a:b], xq_scale_table[:].indirect(entries(offs_l, a, b)))
            if a == 0:
                d_picked = picked_words(d_table, k1_l, "d_words", "d_picked_words")
                d_dealt = deal(d_picked, d_plane, "d_dealt")
            nc.vector.tensor_copy(xq_words[:, a:b], x_table[:].indirect(entries(offs_l, a, b)))
            for t in range(PACK):
                product(h[:, t, a:b], d_dealt[t], xq_words[:, a:b], xq_plane[:, a:b])
                nc.scalar.activation(ds[t][:].indirect(entries(n1_l, a, b)), h[:, t, a:b], COPY)

        x_scale_table = load_scales(nc.sync, x_scales, T, "x_scale_table", "d_table")
        picked_scales(x_scale_table, cand_l, c_plane, nc.sync, "c_scales", "x_picked_scales")
        c_picked = picked_words(x_table, cand_l, "c_words", "x_picked_words")
        c_dealt = deal(c_picked, c_plane, "c_dealt")

        fetched = keep.tile([P, PACK, S], F32, name="fetched")
        z = keep.tile([P, S, PACK], BF16, name="z", align_bytes=64)
        z_words = keep.tile([P, S], U32, name="z_words", align_bytes=64)
        z_plane = keep.tile([P, S], U8, name="z_plane", align_bytes=64)
        s = [keep.tile([P, S], F32, name="s%d" % t) for t in range(PACK)]
        page = [keep.tile([P, U], F32, name="page%d" % t) for t in range(PACK)]
        for j, (a, b) in enumerate(Z_CHUNKS):
            larger = keep.tile([P, PACK, b - a], F32, name="larger%d" % j)
            for t in range(PACK):
                nc.scalar.activation(fetched[:, t, a:b], ds[t][:].indirect(entries(n2_l, a, b)), COPY)
            nc.vector.tensor_tensor(larger[:], h[:, :, a:b], fetched[:, :, a:b], ALU.max)
            nc.vector.tensor_tensor(
                z[:, a:b, :].rearrange("p (c i) t -> p c t i", i=4),
                larger[:].rearrange("p t (c i) -> p c t i", i=4),
                gain[:].unsqueeze(1).unsqueeze(3).to_broadcast([P, (b - a) // 4, PACK, 4]),
                ALU.mult,
            )
            nc.vector.quantize_mx(
                z_words[:, a:b].bitcast(FP8X4), z_plane[:, a:b], z[:, a:b, :].rearrange("p c t -> p (c t)")
            )
            for t in FINISH_ORDER:
                product(s[t][:, a:b], c_dealt[t], z_words[:, a:b], z_plane[:, a:b], sixteenth[:] if j == 0 else 0.0625)

        for a, b in Z_CHUNKS[:-1]:
            for t in range(PACK):
                nc.scalar.activation(page[t][:].indirect(entries(n3_l, a, b)), s[t][:, a:b], COPY)

        partner = [keep.tile([P, S], F32, name="partner%d" % t) for t in range(PACK)]
        nw = [keep.tile([P, S], F32, name="nw%d" % t) for t in range(PACK)]
        left = keep.tile([P, PAGE_SPLIT, PACK], BF16, name="left", align_bytes=64)
        right = keep.tile([P, U - PAGE_SPLIT, PACK], BF16, name="right", align_bytes=64)
        out_rows = out_0.rearrange("(p t) c -> p t c", t=PACK)

        def finish(t):
            nc.scalar.activation(page[t][:].indirect(n4_l[:]), nw[t][:], COPY)
            nc.sync.dma_start(out_rows[:, t, :], page[t][:])
            if t == PACK - 1:
                nc.scalar.copy(right[:, :, t], page[t][:, PAGE_SPLIT:U])
            else:
                nc.vector.tensor_copy(right[:, :, t], page[t][:, PAGE_SPLIT:U])
            nc.vector.tensor_copy(left[:, :, t], page[t][:, 0:PAGE_SPLIT])

        a, b = Z_CHUNKS[-1]
        for n, t in enumerate(FINISH_ORDER):
            nc.scalar.activation(page[t][:].indirect(entries(n3_l, a, b)), s[t][:, a:b], COPY)
            for c, d in HALVES:
                nc.scalar.activation(partner[t][:, c:d], s[t][:].indirect(entries(n5_l, c, d)), COPY)
            nc.vector.tensor_tensor(nw[t][:], s[t][:], partner[t][:], ALU.subtract)
            if n > 0:
                finish(FINISH_ORDER[n - 1])
        finish(PACK - 1)

        o_words = keep.tile([P, U], U32, name="o_words", align_bytes=64)
        o_plane = keep.tile([P, U], U8, name="o_plane", align_bytes=64)
        word_rows = out_1[0].rearrange("p n t -> p (n t)").bitcast(I32)
        for part, a, b in ((left, 0, PAGE_SPLIT), (right, PAGE_SPLIT, U)):
            nc.vector.quantize_mx(o_words[:, a:b].bitcast(FP8X4), o_plane[:, a:b], part[:].rearrange("p c t -> p (c t)"))
            nc.sync.dma_start(word_rows[:, a:b], o_words[:, a:b].bitcast(I32))
        scale_rows = out_2[0].bitcast(I32)
        for q in range(4):
            queue = nc.scalar if q % 2 == 0 else nc.sync
            queue.dma_start(scale_rows[4 * q : 4 * q + 4, :], o_plane[32 * q : 32 * q + 4, :].bitcast(I32))
